import numpy as np
import ml_dtypes


def mxq(x, axis, fmt="e4m3"):
    dtype, down = {"e4m3": (ml_dtypes.float8_e4m3fn, 7), "e5m2": (ml_dtypes.float8_e5m2, 14)}[fmt]
    v = np.moveaxis(np.asarray(x, np.float32).astype(ml_dtypes.bfloat16).astype(np.float64), axis, -1)
    blocks = v.reshape(v.shape[:-1] + (-1, 32))
    amax = np.abs(blocks).max(-1, keepdims=True)
    byte = np.maximum(np.where(amax > 0, np.frexp(amax)[1] - 1 + 127, 0) - down, 1)
    scale = np.exp2(byte - 127.0)
    codes = (blocks / scale).astype(np.float32).astype(dtype).astype(np.float64)
    return np.moveaxis((codes * scale).reshape(v.shape), -1, axis)


WIDE = False


def mx_kscale(k):
    if not WIDE:
        return np.ones(k)
    levels = np.array([10, -10, 5, -5, 0])
    if k % 512:
        return np.exp2(np.random.permutation(np.resize(levels, k // 32))).repeat(32)
    a = np.empty((k // 512, 16))
    for p in range(k // 512):
        a[p, :8] = np.random.permutation(np.resize(levels, 8))
        for g in range(8):
            far = levels[np.abs(levels - a[p, g]) >= 10]
            a[p, g + 8] = far[np.random.randint(len(far))]
    return np.exp2(a.ravel()).repeat(32)


def f64(x):
    return np.asarray(x).astype(np.float64)


def striped(idx):
    return np.tile(idx.reshape(-1, 16).T, (8, 1)).astype(np.uint16)


def unstriped(offs):
    return offs[:16].T.reshape(-1).astype(np.int64)


E2M1 = np.array([0.0, 0.5, 1.0, 1.5, 2.0, 3.0, 4.0, 6.0, -0.0, -0.5, -1.0, -1.5, -2.0, -3.0, -4.0, -6.0])


def pack_weight(w, fmt):
    k, n = w.shape
    w = f64(np.asarray(w, np.float32).astype(ml_dtypes.bfloat16)).reshape(k // 32, 32, n)
    amax = np.abs(w).max(1)
    if fmt == "e4m3":
        byte = np.frexp(amax)[1] - 1 + 127 - 7
    else:
        mant, ex = np.frexp(amax / 6.0)
        byte = np.where(mant > 0.5, ex, ex - 1) + 127
    byte = np.clip(np.where(amax > 0, byte, 1), 1, 254)
    scaled = (w * np.exp2(127.0 - byte)[:, None, :]).reshape(k, n).astype(np.float32)
    by_word = np.ascontiguousarray(scaled.reshape(k // 512, 128, 4, n).transpose(0, 1, 3, 2))
    if fmt == "e4m3":
        words = by_word.astype(ml_dtypes.float8_e4m3fn).view(np.uint8)
    else:
        c = by_word.astype(ml_dtypes.float4_e2m1fn).view(np.uint8) & 0xF
        words = (c[..., 0::2] | (c[..., 1::2] << 4)).reshape(k // 512, 128, 2 * n)
    return np.ascontiguousarray(words), np.ascontiguousarray(byte.astype(np.uint8).reshape(k // 512, 16, n))


def unpack_weight(words, scales, fmt):
    g, _, n = scales.shape
    words = np.ascontiguousarray(words).reshape(g, 128, n, -1)
    if fmt == "e4m3":
        vals = words.view(ml_dtypes.float8_e4m3fn).astype(np.float64)
    else:
        nib = np.empty((g, 128, n, 4), np.uint8)
        nib[..., 0::2] = words & 0xF
        nib[..., 1::2] = words >> 4
        vals = E2M1[nib]
    vals = vals * np.repeat(np.exp2(scales.astype(np.float64) - 127.0), 8, axis=1)[..., None]
    return vals.transpose(0, 1, 3, 2).reshape(g * 512, n)


def gelu(v):
    return 0.5 * v * (1.0 + np.tanh(np.sqrt(2.0 / np.pi) * (v + 0.044715 * v**3)))


K, T, E, C, N = 1536, 1024, 12, 256, 128
TOP = 3


def by_expert(wq, xq):
    return np.concatenate([wq[e].T @ xq[:, e * C:(e + 1) * C] for e in range(E)], axis=1)


def setup_inputs():
    n = np.random.standard_normal
    s = mx_kscale(K)[:, None]
    deal = np.repeat(np.arange(E), C).reshape(TOP, T)[:, np.random.permutation(T)]
    deal = np.take_along_axis(deal, np.argsort(np.random.rand(TOP, T), axis=0), axis=0)
    for _ in range(8):
        s_, t_ = np.random.permutation(T).reshape(2, -1); r = np.random.randint(TOP, size=T // 2); x, y = deal[r, s_].copy(), deal[r, t_].copy()
        ok = ~((deal[:, s_] == y).any(0) | (deal[:, t_] == x).any(0)); deal[r[ok], s_[ok]] = y[ok]; deal[r[ok], t_[ok]] = x[ok]
    order = np.lexsort((np.random.rand(TOP * T), deal.reshape(-1)))
    slot_token = order % T; pos = np.empty(TOP * T, np.int64); pos[order] = np.arange(TOP * T); pos = pos.reshape(TOP, T)
    g = np.random.uniform(0.5, 1.5, (TOP, T)); g = g / g.sum(0)
    x = pack_weight(n((K, T)) * s, "e4m3")
    return {
        "x_words": x[0],
        "x_scales": x[1],
        "w": (n((E + 1, K, N)) / np.sqrt(K) / s[None]).astype(np.float32),
        "b": (0.3 * n((N, E + 1))).astype(np.float32),
        "gate": np.stack([np.tile(r, (N, 1)) for r in g]).astype(np.float32),
        "offs": striped(slot_token),
        "pos1": striped(pos[0]),
        "pos2": striped(pos[1]),
        "pos3": striped(pos[2]),
    }


def reference(x_words, x_scales, w, b, gate, offs, pos1, pos2, pos3):
    idx = unstriped(offs)
    wq = mxq(f64(w), 1, "e4m3")
    xs = unpack_weight(x_words, x_scales, "e4m3")
    ys = gelu((wq[E].T @ xs) + f64(b)[:, E:])
    xq = unpack_weight(x_words, x_scales, "e4m3")[:, idx]
    y = by_expert(wq, xq)
    y = gelu(y + np.repeat(f64(b)[:, :E], C, axis=1))
    return ys + sum(f64(gate[r]) * y[:, unstriped(p)] for r, p in enumerate((pos1, pos2, pos3)))

@@ -1,0 +1,194 @@
+from contextlib import ExitStack
+
+import concourse.mybir as mybir
+from concourse.masks import make_identity
+
+K, T, E, C, N = 1536, 1024, 12, 256, 128
+TOP = 3
+FLOPS = 2 * K * N * (E * C + T)
+BYTES = K * T + K * T // 32 + 4 * (E + 1) * K * N + 4 * N * (E + 1) + 4 * TOP * T + 2 * 128 * (E * C + TOP * T) // 16 + 4 * N * T
+
+F32 = mybir.dt.float32
+BF16 = mybir.dt.bfloat16
+I32 = mybir.dt.int32
+U32 = mybir.dt.uint32
+U16 = mybir.dt.uint16
+U8 = mybir.dt.uint8
+FP8X4 = mybir.dt.float8_e4m3fn_x4
+GELU = mybir.ActivationFunctionType.Gelu_apprx_tanh
+COPY = mybir.ActivationFunctionType.Copy
+ADD = mybir.AluOpType.add
+
+P = 128
+PACK = 4
+PASSES = K // (P * PACK)
+GROUP = 3
+GROUPS = E // GROUP
+SLOTS = GROUP * C
+BANKS = 8
+HALF = 512
+BLOCKS = HALF // P
+
+
+def tile_moe_shr_lin_gelu_kernel(tc, x_words, x_scales, w, b, gate, offs, pos1, pos2, pos3, out):
+    nc = tc.nc
+    with ExitStack() as ctx:
+        lists = ctx.enter_context(tc.tile_pool(name="lists", bufs=1))
+        keep = ctx.enter_context(tc.tile_pool(name="keep", bufs=1))
+        turns = ctx.enter_context(tc.tile_pool(name="turns", bufs=1))
+        psum = ctx.enter_context(tc.psum_pool(name="psum", bufs=1))
+
+        offs_sb = lists.tile([P, E * C // 16], U16, name="offs_sb")
+        pos_sb = [lists.tile([P, T // 16], U16, name=f"pos_sb{r}") for r in range(TOP)]
+        tok_words = [keep.tile([P, T], U32, name=f"tok_words{a}", align_bytes=64) for a in range(PASSES)]
+        tok_scales = keep.tile([P, T], U8, name="tok_scales", align_bytes=64)
+        w_raw = [turns.tile([P, PASSES, PACK, N], F32, name=f"w_raw{e}", tag=f"turn{e}", align_bytes=64) for e in range(E + 1)]
+        bias = keep.tile([P, E + 1], F32, name="bias")
+        gate_rows = keep.tile([P, P], F32, name="gate_rows")
+        gate_cols = keep.tile([P, TOP * T // P], F32, name="gate_cols")
+        ident = keep.tile([P, P], F32, name="ident")
+
+        nc.gpsimd.memset(tok_scales[:].bitcast(I32), 0)
+        nc.gpsimd.memset(gate_rows[:], 0.0)
+        make_identity(nc, ident[:])
+
+        def load_words(a):
+            nc.sync.dma_start(out=tok_words[a][:].bitcast(I32), in_=x_words[a].rearrange("p t r -> p (t r)").bitcast(I32))
+
+        def load_w(e):
+            nc.sync.dma_start(out=w_raw[e][:], in_=w[e].rearrange("(a p j) n -> p a j n", p=P, j=PACK))
+
+        nc.sync.dma_start(offs_sb[:], offs)
+        load_words(0)
+        load_w(0)
+        load_w(1)
+        load_words(1)
+        load_w(2)
+        for q in range(4):
+            nc.sync.dma_start(
+                out=tok_scales[32 * q : 32 * q + 4 * PASSES, :].bitcast(I32),
+                in_=x_scales[:, 4 * q : 4 * q + 4, :].bitcast(I32),
+            )
+        load_w(3)
+        load_words(2)
+        nc.sync.dma_start(out=gate_rows[0 : TOP * T // P, :], in_=gate[:, 0, :].rearrange("r (s t) -> r s t", t=P))
+        load_w(4)
+        nc.sync.dma_start(out=bias[:], in_=b)
+        for e in range(5, E + 1):
+            load_w(e)
+        for r, pos in enumerate((pos1, pos2, pos3)):
+            nc.sync.dma_start(pos_sb[r][:], pos)
+
+        def bank(i, name):
+            return psum.tile([P, HALF], F32, name=name, tag=f"bank{i % BANKS}")
+
+        gate_turned = bank(BANKS - 1, "gate_turned")
+        nc.tensor.transpose(gate_turned[:, 0:P], gate_rows[:], ident[:])
+        nc.scalar.copy(out=gate_cols[:], in_=gate_turned[:, 0 : TOP * T // P])
+
+        slot_words = {}
+        slot_scales = {}
+
+        def gather(kind, g, tag, cuts=1):
+            pool = turns if tag.startswith("turn") else keep
+            if kind == "scales":
+                dst = pool.tile([P, SLOTS], U8, name=f"slot_scales{g}", tag=tag, align_bytes=64)
+                slot_scales[g] = dst
+                src = tok_scales
+            else:
+                dst = pool.tile([P, SLOTS], U32, name=f"slot_words{kind}_{g}", tag=tag, align_bytes=64)
+                slot_words[kind, g] = dst
+                src = tok_words[kind]
+            width = SLOTS // cuts
+            for i in range(cuts):
+                first = g * SLOTS + i * width
+                nc.vector.tensor_copy(dst[:, i * width : (i + 1) * width], src[:].indirect(offs_sb[:, first // 16 : (first + width) // 16]))
+
+        w_bf = [keep.tile([P, PASSES * N * PACK], BF16, name=f"w_bf{e}", align_bytes=64) for e in range(E + 1)]
+        w_codes = [keep.tile([P, PASSES * N], U32, name=f"w_codes{e}", align_bytes=64) for e in range(E + 1)]
+        w_scales = [keep.tile([P, PASSES * N], U8, name=f"w_scales{e}", align_bytes=64) for e in range(E + 1)]
+
+        def cast(e):
+            nc.scalar.copy(
+                out=w_bf[e][:].rearrange("p (a c i t) -> p a c t i", a=PASSES, i=4, t=PACK),
+                in_=w_raw[e][:].rearrange("p a t (c i) -> p a c t i", i=4),
+            )
+
+        def quantize(e):
+            for lo, hi in ((0, 2 * N), (2 * N, 3 * N)):
+                nc.vector.quantize_mx(
+                    out=w_codes[e][:, lo:hi].bitcast(FP8X4),
+                    scales=w_scales[e][:, lo:hi],
+                    in_=w_bf[e][:, PACK * lo : PACK * hi],
+                )
+
+        def product(acc, e, words, scales, cols):
+            for a in range(PASSES):
+                nc.tensor.matmul_mx(
+                    out=acc,
+                    lhsT=w_codes[e][:, a * N : (a + 1) * N].bitcast(FP8X4),
+                    lhsT_scale=w_scales[e][:, a * N : (a + 1) * N],
+                    rhs=words[a][:, cols].bitcast(FP8X4),
+                    rhs_scale=scales[4 * a : P, cols],
+                    start=(a == 0),
+                    stop=(a == PASSES - 1),
+                )
+
+        for g in range(GROUPS):
+            gather(0, g, f"head{g}")
+        later = [(1, g) for g in range(GROUPS)]
+        for g in range(GROUPS):
+            later.extend([("scales", g), (2, g)])
+        turn_of = list(range(E - 1)) + [E]
+        todo = dict(zip(turn_of, later))
+        for e in range(E + 1):
+            cast(e)
+            if e in todo:
+                kind, g = todo[e]
+                gather(kind, g, f"turn{e}", cuts=GROUP if e == E else 1)
+            quantize(e)
+
+        y = turns.tile([P, E * C], F32, name="y", tag=f"turn{E - 1}", align_bytes=64)
+        for e in range(E):
+            g, i = divmod(e, GROUP)
+            acc = bank(e, f"acc{e}")
+            product(acc[:, 0:C], e, [slot_words[a, g] for a in range(PASSES)], slot_scales[g], slice(i * C, (i + 1) * C))
+            nc.scalar.activation(out=y[:, e * C : (e + 1) * C], in_=acc[:, 0:C], func=GELU, bias=bias[:, e : e + 1])
+
+        ys = [keep.tile([P, HALF], F32, name=f"ys{h}") for h in range(T // HALF)]
+        for h in range(T // HALF):
+            acc = bank(E + h, f"acc_shared{h}")
+            product(acc[:], E, tok_words, tok_scales, slice(h * HALF, (h + 1) * HALF))
+            nc.scalar.activation(out=ys[h][:], in_=acc[:], func=GELU, bias=bias[:, E : E + 1])
+
+        fwd_bank = [[6, 7, 0], [2, 3, 6]]
+        sum_bank = [1, 7]
+        sums = []
+        for h in range(T // HALF):
+            total = bank(sum_bank[h], f"total{h}")
+            sums.append(total)
+            for r in range(TOP):
+                picked = keep.tile([P, HALF], F32, name=f"picked{h}_{r}")
+                nc.vector.tensor_copy(picked[:], y[:].indirect(pos_sb[r][:, h * HALF // 16 : (h + 1) * HALF // 16]))
+                turned = bank(fwd_bank[h][r], f"turned{h}_{r}")
+                for s in range(BLOCKS):
+                    nc.tensor.transpose(turned[:, s * P : (s + 1) * P], picked[:, s * P : (s + 1) * P], ident[:])
+                gated = keep.tile([P, HALF], F32, name=f"gated{h}_{r}")
+                for s in range(BLOCKS):
+                    col = r * (T // P) + h * BLOCKS + s
+                    nc.scalar.activation(
+                        out=gated[:, s * P : (s + 1) * P], in_=turned[:, s * P : (s + 1) * P], func=COPY, scale=gate_cols[:, col : col + 1]
+                    )
+                for s in range(BLOCKS):
+                    nc.tensor.matmul(
+                        total[:, s * P : (s + 1) * P],
+                        lhsT=gated[:, s * P : (s + 1) * P],
+                        rhs=ident[:],
+                        start=(r == 0 and s == 0),
+                        stop=(r == TOP - 1 and s == BLOCKS - 1),
+                        is_transpose=True,
+                    )
+        for h in range(T // HALF):
+            result = keep.tile([P, HALF], F32, name=f"result{h}")
+            nc.vector.tensor_tensor(out=result[:], in0=sums[h][:], in1=ys[h][:], op=ADD)
+            nc.sync.dma_start(out=out[:, h * HALF : (h + 1) * HALF], in_=result[:])

@@ -16,8 +16,8 @@ U16 = mybir.dt.uint16
 U8 = mybir.dt.uint8
 FP8X4 = mybir.dt.float8_e4m3fn_x4
 GELU = mybir.ActivationFunctionType.Gelu_apprx_tanh
-COPY = mybir.ActivationFunctionType.Copy
 ADD = mybir.AluOpType.add
+MULT = mybir.AluOpType.mult
 
 P = 128
 PACK = 4
@@ -44,12 +44,10 @@ def tile_moe_shr_lin_gelu_kernel(tc, x_words, x_scales, w, b, gate, offs, pos1, 
         tok_scales = keep.tile([P, T], U8, name="tok_scales", align_bytes=64)
         w_raw = [turns.tile([P, PASSES, PACK, N], F32, name=f"w_raw{e}", tag=f"turn{e}", align_bytes=64) for e in range(E + 1)]
         bias = keep.tile([P, E + 1], F32, name="bias")
-        gate_rows = keep.tile([P, P], F32, name="gate_rows")
-        gate_cols = keep.tile([P, TOP * T // P], F32, name="gate_cols")
+        gate_sb = [keep.tile([P, T], F32, name=f"gate_sb{r}") for r in range(TOP)]
         ident = keep.tile([P, P], F32, name="ident")
 
         nc.gpsimd.memset(tok_scales[:].bitcast(I32), 0)
-        nc.gpsimd.memset(gate_rows[:], 0.0)
         make_identity(nc, ident[:])
 
         def load_words(a):
@@ -58,8 +56,8 @@ def tile_moe_shr_lin_gelu_kernel(tc, x_words, x_scales, w, b, gate, offs, pos1, 
         def load_w(e):
             nc.sync.dma_start(out=w_raw[e][:], in_=w[e].rearrange("(a p j) n -> p a j n", p=P, j=PACK))
 
-        nc.sync.dma_start(offs_sb[:], offs)
         load_words(0)
+        nc.sync.dma_start(offs_sb[:], offs)
         load_w(0)
         load_w(1)
         load_words(1)
@@ -71,25 +69,21 @@ def tile_moe_shr_lin_gelu_kernel(tc, x_words, x_scales, w, b, gate, offs, pos1, 
             )
         load_w(3)
         load_words(2)
-        nc.sync.dma_start(out=gate_rows[0 : TOP * T // P, :], in_=gate[:, 0, :].rearrange("r (s t) -> r s t", t=P))
         load_w(4)
         nc.sync.dma_start(out=bias[:], in_=b)
         for e in range(5, E + 1):
             load_w(e)
         for r, pos in enumerate((pos1, pos2, pos3)):
             nc.sync.dma_start(pos_sb[r][:], pos)
+            nc.sync.dma_start(out=gate_sb[r][:], in_=gate[r])
 
         def bank(i, name):
             return psum.tile([P, HALF], F32, name=name, tag=f"bank{i % BANKS}")
 
-        gate_turned = bank(BANKS - 1, "gate_turned")
-        nc.tensor.transpose(gate_turned[:, 0:P], gate_rows[:], ident[:])
-        nc.scalar.copy(out=gate_cols[:], in_=gate_turned[:, 0 : TOP * T // P])
-
         slot_words = {}
         slot_scales = {}
 
-        def gather(kind, g, tag, cuts=1):
+        def gather(kind, g, tag, widths=(SLOTS,)):
             pool = turns if tag.startswith("turn") else keep
             if kind == "scales":
                 dst = pool.tile([P, SLOTS], U8, name=f"slot_scales{g}", tag=tag, align_bytes=64)
@@ -99,10 +93,11 @@ def tile_moe_shr_lin_gelu_kernel(tc, x_words, x_scales, w, b, gate, offs, pos1, 
                 dst = pool.tile([P, SLOTS], U32, name=f"slot_words{kind}_{g}", tag=tag, align_bytes=64)
                 slot_words[kind, g] = dst
                 src = tok_words[kind]
-            width = SLOTS // cuts
-            for i in range(cuts):
-                first = g * SLOTS + i * width
-                nc.vector.tensor_copy(dst[:, i * width : (i + 1) * width], src[:].indirect(offs_sb[:, first // 16 : (first + width) // 16]))
+            lo = 0
+            for width in widths:
+                first = g * SLOTS + lo
+                nc.vector.tensor_copy(dst[:, lo : lo + width], src[:].indirect(offs_sb[:, first // 16 : (first + width) // 16]))
+                lo = lo + width
 
         w_bf = [keep.tile([P, PASSES * N * PACK], BF16, name=f"w_bf{e}", align_bytes=64) for e in range(E + 1)]
         w_codes = [keep.tile([P, PASSES * N], U32, name=f"w_codes{e}", align_bytes=64) for e in range(E + 1)]
@@ -145,50 +140,58 @@ def tile_moe_shr_lin_gelu_kernel(tc, x_words, x_scales, w, b, gate, offs, pos1, 
             cast(e)
             if e in todo:
                 kind, g = todo[e]
-                gather(kind, g, f"turn{e}", cuts=GROUP if e == E else 1)
+                gather(kind, g, f"turn{e}", widths=(C, C, C // 2, C // 2) if e == E else (SLOTS,))
             quantize(e)
 
         y = turns.tile([P, E * C], F32, name="y", tag=f"turn{E - 1}", align_bytes=64)
-        for e in range(E):
+        pieces = [(e, 0, C) for e in range(E - 1)] + [(E - 1, 0, C // 2), (E - 1, C // 2, C // 2)]
+        for j, (e, lo, width) in enumerate(pieces):
             g, i = divmod(e, GROUP)
-            acc = bank(e, f"acc{e}")
-            product(acc[:, 0:C], e, [slot_words[a, g] for a in range(PASSES)], slot_scales[g], slice(i * C, (i + 1) * C))
-            nc.scalar.activation(out=y[:, e * C : (e + 1) * C], in_=acc[:, 0:C], func=GELU, bias=bias[:, e : e + 1])
+            acc = bank(j, f"acc{j}")
+            product(acc[:, 0:width], e, [slot_words[a, g] for a in range(PASSES)], slot_scales[g], slice(i * C + lo, i * C + lo + width))
+            nc.scalar.activation(out=y[:, e * C + lo : e * C + lo + width], in_=acc[:, 0:width], func=GELU, bias=bias[:, e : e + 1])
 
         ys = [keep.tile([P, HALF], F32, name=f"ys{h}") for h in range(T // HALF)]
         for h in range(T // HALF):
-            acc = bank(E + h, f"acc_shared{h}")
+            acc = bank(5 + h, f"acc_shared{h}")
             product(acc[:], E, tok_words, tok_scales, slice(h * HALF, (h + 1) * HALF))
             nc.scalar.activation(out=ys[h][:], in_=acc[:], func=GELU, bias=bias[:, E : E + 1])
 
-        fwd_bank = [[6, 7, 0], [2, 3, 6]]
-        sum_bank = [1, 7]
-        sums = []
+        def gated(h, r):
+            term = keep.tile([P, HALF], F32, name=f"term{h}_{r}")
+            cols = slice(h * HALF, (h + 1) * HALF)
+            nc.vector.tensor_tensor(
+                out=term[:], in0=y[:].indirect(pos_sb[r][:, h * HALF // 16 : (h + 1) * HALF // 16]), in1=gate_sb[r][:, cols], op=MULT
+            )
+            return term
+
+        def turn(dst, src, blocks, start, stop):
+            for s in blocks:
+                nc.tensor.matmul(
+                    dst[:, s * P : (s + 1) * P],
+                    lhsT=src[:, s * P : (s + 1) * P],
+                    rhs=ident[:],
+                    start=(start and s == 0),
+                    stop=(stop and s == BLOCKS - 1),
+                    is_transpose=True,
+                )
+
+        totals = []
         for h in range(T // HALF):
-            total = bank(sum_bank[h], f"total{h}")
-            sums.append(total)
-            for r in range(TOP):
-                picked = keep.tile([P, HALF], F32, name=f"picked{h}_{r}")
-                nc.vector.tensor_copy(picked[:], y[:].indirect(pos_sb[r][:, h * HALF // 16 : (h + 1) * HALF // 16]))
-                turned = bank(fwd_bank[h][r], f"turned{h}_{r}")
-                for s in range(BLOCKS):
-                    nc.tensor.transpose(turned[:, s * P : (s + 1) * P], picked[:, s * P : (s + 1) * P], ident[:])
-                gated = keep.tile([P, HALF], F32, name=f"gated{h}_{r}")
-                for s in range(BLOCKS):
-                    col = r * (T // P) + h * BLOCKS + s
-                    nc.scalar.activation(
-                        out=gated[:, s * P : (s + 1) * P], in_=turned[:, s * P : (s + 1) * P], func=COPY, scale=gate_cols[:, col : col + 1]
-                    )
-                for s in range(BLOCKS):
-                    nc.tensor.matmul(
-                        total[:, s * P : (s + 1) * P],
-                        lhsT=gated[:, s * P : (s + 1) * P],
-                        rhs=ident[:],
-                        start=(r == 0 and s == 0),
-                        stop=(r == TOP - 1 and s == BLOCKS - 1),
-                        is_transpose=True,
-                    )
-        for h in range(T // HALF):
-            result = keep.tile([P, HALF], F32, name=f"result{h}")
-            nc.vector.tensor_tensor(out=result[:], in0=sums[h][:], in1=ys[h][:], op=ADD)
-            nc.sync.dma_start(out=out[:, h * HALF : (h + 1) * HALF], in_=result[:])
+            turned = bank(7 + h, f"turned{h}")
+            turn(turned, gated(h, 0), range(BLOCKS), True, False)
+            turn(turned, ys[h], range(BLOCKS), False, False)
+            turn(turned, gated(h, 1), range(BLOCKS), False, True)
+            total = bank(1 + h, f"total{h}")
+            totals.append(total)
+            summed = keep.tile([P, HALF], F32, name=f"summed{h}")
+            for blocks in (range(0, 2), range(2, BLOCKS)):
+                cols = slice(blocks.start * P, blocks.stop * P)
+                nc.scalar.copy(out=summed[:, cols], in_=turned[:, cols])
+                turn(total, summed, blocks, True, True)
+        thirds = [gated(h, TOP - 1) for h in range(T // HALF)]
+        for lo, width, queue in ((0, HALF, nc.sync), (HALF, HALF // 2, nc.scalar), (HALF + HALF // 2, HALF // 2, nc.sync)):
+            h, at = divmod(lo, HALF)
+            result = keep.tile([P, width], F32, name=f"result{lo}")
+            nc.vector.tensor_tensor(out=result[:], in0=totals[h][:, at : at + width], in1=thirds[h][:, at : at + width], op=ADD)
+            queue.dma_start(out=out[:, lo : lo + width], in_=result[:])

@@ -99,30 +99,36 @@ def tile_moe_shr_lin_gelu_kernel(tc, x_words, x_scales, w, b, gate, offs, pos1, 
                 nc.vector.tensor_copy(dst[:, lo : lo + width], src[:].indirect(offs_sb[:, first // 16 : (first + width) // 16]))
                 lo = lo + width
 
-        w_bf = [keep.tile([P, PASSES * N * PACK], BF16, name=f"w_bf{e}", align_bytes=64) for e in range(E + 1)]
-        w_codes = [keep.tile([P, PASSES * N], U32, name=f"w_codes{e}", align_bytes=64) for e in range(E + 1)]
-        w_scales = [keep.tile([P, PASSES * N], U8, name=f"w_scales{e}", align_bytes=64) for e in range(E + 1)]
+        wide = PASSES * N
+        sizes = [GROUP * wide] * GROUPS + [wide]
+        w_bf = [keep.tile([P, size * PACK], BF16, name=f"w_bf{g}", align_bytes=64) for g, size in enumerate(sizes)]
+        w_codes = [keep.tile([P, size], U32, name=f"w_codes{g}", align_bytes=64) for g, size in enumerate(sizes)]
+        w_scales = [keep.tile([P, size], U8, name=f"w_scales{g}", align_bytes=64) for g, size in enumerate(sizes)]
 
         def cast(e):
+            g, i = divmod(e, GROUP)
             nc.scalar.copy(
-                out=w_bf[e][:].rearrange("p (a c i t) -> p a c t i", a=PASSES, i=4, t=PACK),
+                out=w_bf[g][:, i * wide * PACK : (i + 1) * wide * PACK].rearrange("p (a c i t) -> p a c t i", a=PASSES, i=4, t=PACK),
                 in_=w_raw[e][:].rearrange("p a t (c i) -> p a c t i", i=4),
             )
 
-        def quantize(e):
-            for lo, hi in ((0, 2 * N), (2 * N, 3 * N)):
+        def quantize(g):
+            cut = sizes[g] - N
+            for lo, hi in ((0, cut), (cut, sizes[g])):
                 nc.vector.quantize_mx(
-                    out=w_codes[e][:, lo:hi].bitcast(FP8X4),
-                    scales=w_scales[e][:, lo:hi],
-                    in_=w_bf[e][:, PACK * lo : PACK * hi],
+                    out=w_codes[g][:, lo:hi].bitcast(FP8X4),
+                    scales=w_scales[g][:, lo:hi],
+                    in_=w_bf[g][:, PACK * lo : PACK * hi],
                 )
 
         def product(acc, e, words, scales, cols):
+            g, i = divmod(e, GROUP)
             for a in range(PASSES):
+                w_cols = slice(i * wide + a * N, i * wide + (a + 1) * N)
                 nc.tensor.matmul_mx(
                     out=acc,
-                    lhsT=w_codes[e][:, a * N : (a + 1) * N].bitcast(FP8X4),
-                    lhsT_scale=w_scales[e][:, a * N : (a + 1) * N],
+                    lhsT=w_codes[g][:, w_cols].bitcast(FP8X4),
+                    lhsT_scale=w_scales[g][:, w_cols],
                     rhs=words[a][:, cols].bitcast(FP8X4),
                     rhs_scale=scales[4 * a : P, cols],
                     start=(a == 0),
@@ -141,7 +147,8 @@ def tile_moe_shr_lin_gelu_kernel(tc, x_words, x_scales, w, b, gate, offs, pos1, 
             if e in todo:
                 kind, g = todo[e]
                 gather(kind, g, f"turn{e}", widths=(C, C, C // 2, C // 2) if e == E else (SLOTS,))
-            quantize(e)
+            if e % GROUP == GROUP - 1 or e == E:
+                quantize(e // GROUP)
 
         y = turns.tile([P, E * C], F32, name="y", tag=f"turn{E - 1}", align_bytes=64)
         pieces = [(e, 0, C) for e in range(E - 1)] + [(E - 1, 0, C // 2), (E - 1, C // 2, C // 2)]
@@ -157,41 +164,52 @@ def tile_moe_shr_lin_gelu_kernel(tc, x_words, x_scales, w, b, gate, offs, pos1, 
             product(acc[:], E, tok_words, tok_scales, slice(h * HALF, (h + 1) * HALF))
             nc.scalar.activation(out=ys[h][:], in_=acc[:], func=GELU, bias=bias[:, E : E + 1])
 
-        def gated(h, r):
-            term = keep.tile([P, HALF], F32, name=f"term{h}_{r}")
-            cols = slice(h * HALF, (h + 1) * HALF)
+        def gated(r, lo, width):
+            term = keep.tile([P, width], F32, name=f"term{r}_{lo}")
             nc.vector.tensor_tensor(
-                out=term[:], in0=y[:].indirect(pos_sb[r][:, h * HALF // 16 : (h + 1) * HALF // 16]), in1=gate_sb[r][:, cols], op=MULT
+                out=term[:], in0=y[:].indirect(pos_sb[r][:, lo // 16 : (lo + width) // 16]), in1=gate_sb[r][:, lo : lo + width], op=MULT
             )
             return term
 
         def turn(dst, src, blocks, start, stop):
-            for s in blocks:
+            for s in range(blocks.start, blocks.stop):
                 nc.tensor.matmul(
                     dst[:, s * P : (s + 1) * P],
                     lhsT=src[:, s * P : (s + 1) * P],
                     rhs=ident[:],
-                    start=(start and s == 0),
-                    stop=(stop and s == BLOCKS - 1),
+                    start=(start and s == blocks.start),
+                    stop=(stop and s == blocks.stop - 1),
                     is_transpose=True,
                 )
 
+        spans = ((0, HALF, nc.sync), (HALF, HALF // 2, nc.scalar), (HALF + HALF // 2, HALF // 2, nc.sync))
         totals = []
         for h in range(T // HALF):
-            turned = bank(7 + h, f"turned{h}")
-            turn(turned, gated(h, 0), range(BLOCKS), True, False)
-            turn(turned, ys[h], range(BLOCKS), False, False)
-            turn(turned, gated(h, 1), range(BLOCKS), False, True)
-            total = bank(1 + h, f"total{h}")
-            totals.append(total)
-            summed = keep.tile([P, HALF], F32, name=f"summed{h}")
-            for blocks in (range(0, 2), range(2, BLOCKS)):
-                cols = slice(blocks.start * P, blocks.stop * P)
-                nc.scalar.copy(out=summed[:, cols], in_=turned[:, cols])
-                turn(total, summed, blocks, True, True)
-        thirds = [gated(h, TOP - 1) for h in range(T // HALF)]
-        for lo, width, queue in ((0, HALF, nc.sync), (HALF, HALF // 2, nc.scalar), (HALF + HALF // 2, HALF // 2, nc.sync)):
+            mine = [j for j in range(len(spans)) if spans[j][0] // HALF == h]
+            first = gated(0, h * HALF, HALF)
+            turned = {}
+            for j in mine:
+                lo, width, queue = spans[j]
+                at = lo - h * HALF
+                blocks = range(width // P)
+                turned[j] = bank(7 + j, f"turned{j}")
+                early = [first[:, at : at + width], ys[h][:, at : at + width]]
+                turn(turned[j], early[h], blocks, True, False)
+                turn(turned[j], early[1 - h], blocks, False, False)
+            for j in mine:
+                lo, width, queue = spans[j]
+                turn(turned[j], gated(1, lo, width), range(width // P), False, True)
+            for j in mine:
+                lo, width, queue = spans[j]
+                total = bank(2 + j, f"total{j}")
+                totals.append(total)
+                summed = keep.tile([P, width], F32, name=f"summed{j}")
+                for s in range(0, width // P, 2):
+                    nc.scalar.copy(out=summed[:, s * P : (s + 2) * P], in_=turned[j][:, s * P : (s + 2) * P])
+                    turn(total, summed, range(s, s + 2), s == 0, s + 2 == width // P)
+        thirds = [gated(TOP - 1, h * HALF, HALF) for h in range(T // HALF)]
+        for j, (lo, width, queue) in enumerate(spans):
             h, at = divmod(lo, HALF)
             result = keep.tile([P, width], F32, name=f"result{lo}")
-            nc.vector.tensor_tensor(out=result[:], in0=totals[h][:, at : at + width], in1=thirds[h][:, at : at + width], op=ADD)
+            nc.vector.tensor_tensor(out=result[:], in0=totals[j][:, 0:width], in1=thirds[h][:, at : at + width], op=ADD)
             queue.dma_start(out=out[:, lo : lo + width], in_=result[:])

from contextlib import ExitStack

import concourse.mybir as mybir
from concourse.masks import make_identity

K, T, E, C, N = 1536, 1024, 12, 256, 128
TOP = 3
FLOPS = 2 * K * N * (E * C + T)
BYTES = K * T + K * T // 32 + 4 * (E + 1) * K * N + 4 * N * (E + 1) + 4 * TOP * T + 2 * 128 * (E * C + TOP * T) // 16 + 4 * N * T

F32 = mybir.dt.float32
BF16 = mybir.dt.bfloat16
I32 = mybir.dt.int32
U32 = mybir.dt.uint32
U16 = mybir.dt.uint16
U8 = mybir.dt.uint8
FP8X4 = mybir.dt.float8_e4m3fn_x4
GELU = mybir.ActivationFunctionType.Gelu_apprx_tanh
ADD = mybir.AluOpType.add
MULT = mybir.AluOpType.mult

P = 128
PACK = 4
PASSES = K // (P * PACK)
GROUP = 3
GROUPS = E // GROUP
SLOTS = GROUP * C
BANKS = 8
HALF = 512
BLOCKS = HALF // P


def tile_moe_shr_lin_gelu_kernel(tc, x_words, x_scales, w, b, gate, offs, pos1, pos2, pos3, out):
    nc = tc.nc
    with ExitStack() as ctx:
        lists = ctx.enter_context(tc.tile_pool(name="lists", bufs=1))
        keep = ctx.enter_context(tc.tile_pool(name="keep", bufs=1))
        turns = ctx.enter_context(tc.tile_pool(name="turns", bufs=1))
        psum = ctx.enter_context(tc.psum_pool(name="psum", bufs=1))

        offs_sb = lists.tile([P, E * C // 16], U16, name="offs_sb")
        pos_sb = [lists.tile([P, T // 16], U16, name=f"pos_sb{r}") for r in range(TOP)]
        tok_words = [keep.tile([P, T], U32, name=f"tok_words{a}", align_bytes=64) for a in range(PASSES)]
        tok_scales = keep.tile([P, T], U8, name="tok_scales", align_bytes=64)
        w_raw = [turns.tile([P, PASSES, PACK, N], F32, name=f"w_raw{e}", tag=f"turn{e}", align_bytes=64) for e in range(E + 1)]
        bias = keep.tile([P, E + 1], F32, name="bias")
        gate_sb = [keep.tile([P, T], F32, name=f"gate_sb{r}") for r in range(TOP)]
        ident = keep.tile([P, P], F32, name="ident")

        nc.gpsimd.memset(tok_scales[:].bitcast(I32), 0)
        make_identity(nc, ident[:])

        def load_words(a):
            nc.sync.dma_start(out=tok_words[a][:].bitcast(I32), in_=x_words[a].rearrange("p t r -> p (t r)").bitcast(I32))

        def load_w(e):
            nc.sync.dma_start(out=w_raw[e][:], in_=w[e].rearrange("(a p j) n -> p a j n", p=P, j=PACK))

        load_words(0)
        nc.sync.dma_start(offs_sb[:], offs)
        load_w(0)
        load_w(1)
        load_words(1)
        load_w(2)
        for q in range(4):
            nc.sync.dma_start(
                out=tok_scales[32 * q : 32 * q + 4 * PASSES, :].bitcast(I32),
                in_=x_scales[:, 4 * q : 4 * q + 4, :].bitcast(I32),
            )
        load_w(3)
        load_words(2)
        load_w(4)
        nc.sync.dma_start(out=bias[:], in_=b)
        for e in range(5, E + 1):
            load_w(e)
        for r, pos in enumerate((pos1, pos2, pos3)):
            nc.sync.dma_start(pos_sb[r][:], pos)
            nc.sync.dma_start(out=gate_sb[r][:], in_=gate[r])

        def bank(i, name):
            return psum.tile([P, HALF], F32, name=name, tag=f"bank{i % BANKS}")

        slot_words = {}
        slot_scales = {}

        def gather(kind, g, tag, widths=(SLOTS,)):
            pool = turns if tag.startswith("turn") else keep
            if kind == "scales":
                dst = pool.tile([P, SLOTS], U8, name=f"slot_scales{g}", tag=tag, align_bytes=64)
                slot_scales[g] = dst
                src = tok_scales
            else:
                dst = pool.tile([P, SLOTS], U32, name=f"slot_words{kind}_{g}", tag=tag, align_bytes=64)
                slot_words[kind, g] = dst
                src = tok_words[kind]
            lo = 0
            for width in widths:
                first = g * SLOTS + lo
                nc.vector.tensor_copy(dst[:, lo : lo + width], src[:].indirect(offs_sb[:, first // 16 : (first + width) // 16]))
                lo = lo + width

        wide = PASSES * N
        sizes = [GROUP * wide] * GROUPS + [wide]
        w_bf = [keep.tile([P, size * PACK], BF16, name=f"w_bf{g}", align_bytes=64) for g, size in enumerate(sizes)]
        w_codes = [keep.tile([P, size], U32, name=f"w_codes{g}", align_bytes=64) for g, size in enumerate(sizes)]
        w_scales = [keep.tile([P, size], U8, name=f"w_scales{g}", align_bytes=64) for g, size in enumerate(sizes)]

        def cast(e):
            g, i = divmod(e, GROUP)
            nc.scalar.copy(
                out=w_bf[g][:, i * wide * PACK : (i + 1) * wide * PACK].rearrange("p (a c i t) -> p a c t i", a=PASSES, i=4, t=PACK),
                in_=w_raw[e][:].rearrange("p a t (c i) -> p a c t i", i=4),
            )

        def quantize(g):
            cut = sizes[g] - N
            for lo, hi in ((0, cut), (cut, sizes[g])):
                nc.vector.quantize_mx(
                    out=w_codes[g][:, lo:hi].bitcast(FP8X4),
                    scales=w_scales[g][:, lo:hi],
                    in_=w_bf[g][:, PACK * lo : PACK * hi],
                )

        def product(acc, e, words, scales, cols):
            g, i = divmod(e, GROUP)
            for a in range(PASSES):
                w_cols = slice(i * wide + a * N, i * wide + (a + 1) * N)
                nc.tensor.matmul_mx(
                    out=acc,
                    lhsT=w_codes[g][:, w_cols].bitcast(FP8X4),
                    lhsT_scale=w_scales[g][:, w_cols],
                    rhs=words[a][:, cols].bitcast(FP8X4),
                    rhs_scale=scales[4 * a : P, cols],
                    start=(a == 0),
                    stop=(a == PASSES - 1),
                )

        for g in range(GROUPS):
            gather(0, g, f"head{g}")
        later = [(1, g) for g in range(GROUPS)]
        for g in range(GROUPS):
            later.extend([("scales", g), (2, g)])
        turn_of = list(range(E - 1)) + [E]
        todo = dict(zip(turn_of, later))
        for e in range(E + 1):
            cast(e)
            if e in todo:
                kind, g = todo[e]
                gather(kind, g, f"turn{e}", widths=(C, C, C // 2, C // 2) if e == E else (SLOTS,))
            if e % GROUP == GROUP - 1 or e == E:
                quantize(e // GROUP)

        y = turns.tile([P, E * C], F32, name="y", tag=f"turn{E - 1}", align_bytes=64)
        pieces = [(e, 0, C) for e in range(E - 1)] + [(E - 1, 0, C // 2), (E - 1, C // 2, C // 2)]
        for j, (e, lo, width) in enumerate(pieces):
            g, i = divmod(e, GROUP)
            acc = bank(j, f"acc{j}")
            product(acc[:, 0:width], e, [slot_words[a, g] for a in range(PASSES)], slot_scales[g], slice(i * C + lo, i * C + lo + width))
            nc.scalar.activation(out=y[:, e * C + lo : e * C + lo + width], in_=acc[:, 0:width], func=GELU, bias=bias[:, e : e + 1])

        ys = [keep.tile([P, HALF], F32, name=f"ys{h}") for h in range(T // HALF)]
        for h in range(T // HALF):
            acc = bank(5 + h, f"acc_shared{h}")
            product(acc[:], E, tok_words, tok_scales, slice(h * HALF, (h + 1) * HALF))
            nc.scalar.activation(out=ys[h][:], in_=acc[:], func=GELU, bias=bias[:, E : E + 1])

        def gated(r, lo, width):
            term = keep.tile([P, width], F32, name=f"term{r}_{lo}")
            nc.vector.tensor_tensor(
                out=term[:], in0=y[:].indirect(pos_sb[r][:, lo // 16 : (lo + width) // 16]), in1=gate_sb[r][:, lo : lo + width], op=MULT
            )
            return term

        def turn(dst, src, blocks, start, stop):
            for s in range(blocks.start, blocks.stop):
                nc.tensor.matmul(
                    dst[:, s * P : (s + 1) * P],
                    lhsT=src[:, s * P : (s + 1) * P],
                    rhs=ident[:],
                    start=(start and s == blocks.start),
                    stop=(stop and s == blocks.stop - 1),
                    is_transpose=True,
                )

        spans = ((0, HALF, nc.sync), (HALF, HALF // 2, nc.scalar), (HALF + HALF // 2, HALF // 2, nc.sync))
        totals = []
        for h in range(T // HALF):
            mine = [j for j in range(len(spans)) if spans[j][0] // HALF == h]
            first = gated(0, h * HALF, HALF)
            turned = {}
            for j in mine:
                lo, width, queue = spans[j]
                at = lo - h * HALF
                blocks = range(width // P)
                turned[j] = bank(7 + j, f"turned{j}")
                early = [first[:, at : at + width], ys[h][:, at : at + width]]
                turn(turned[j], early[h], blocks, True, False)
                turn(turned[j], early[1 - h], blocks, False, False)
            for j in mine:
                lo, width, queue = spans[j]
                turn(turned[j], gated(1, lo, width), range(width // P), False, True)
            for j in mine:
                lo, width, queue = spans[j]
                total = bank(2 + j, f"total{j}")
                totals.append(total)
                summed = keep.tile([P, width], F32, name=f"summed{j}")
                for s in range(0, width // P, 2):
                    nc.scalar.copy(out=summed[:, s * P : (s + 2) * P], in_=turned[j][:, s * P : (s + 2) * P])
                    turn(total, summed, range(s, s + 2), s == 0, s + 2 == width // P)
        thirds = [gated(TOP - 1, h * HALF, HALF) for h in range(T // HALF)]
        for j, (lo, width, queue) in enumerate(spans):
            h, at = divmod(lo, HALF)
            result = keep.tile([P, width], F32, name=f"result{lo}")
            nc.vector.tensor_tensor(out=result[:], in0=totals[j][:, 0:width], in1=thirds[h][:, at : at + width], op=ADD)
            queue.dma_start(out=out[:, lo : lo + width], in_=result[:])
